import numpy as np, ml_dtypes
CORES = [24,25,26,27,28,29,30,31,224,225,226,227,228,229,230,231]
N = 16
W = 32
def setup_inputs(rng):
    return {"x": rng.standard_normal((N, 128, W), dtype=np.float32).astype(ml_dtypes.bfloat16), "a": (7 + rng.standard_normal((N, 128, W), dtype=np.float32) - 9 * (rng.random((N, 128, W)) < 2.0 / (N * W))).astype(ml_dtypes.bfloat16)}
def setup_inputs_big(rng):
    d = setup_inputs(rng)
    for k in ("x",): d[k] = (d[k].astype(np.float32) * 1048576.0).astype(d[k].dtype)
    return d
def setup_inputs_small(rng):
    d = setup_inputs(rng)
    for k in ("x",): d[k] = (d[k].astype(np.float32) * (1 / 1048576.0)).astype(d[k].dtype)
    return d
def setup_inputs_apart(rng):
    d = setup_inputs(rng)
    f = (10.0 ** rng.permutation(np.linspace(-1.5, 1.5, N))).astype(np.float32).reshape(N, 1, 1)
    for k in ("x",): d[k] = (d[k].astype(np.float32) * f).astype(d[k].dtype)
    return d
def reference(x, a):
    X = np.concatenate(list(x.astype(np.float64)), axis=1); G = 1.0 / (1.0 + np.exp(-np.concatenate(list(a.astype(np.float64)), axis=1)))
    h = np.zeros(128); H = np.zeros_like(X)
    for c in range(N * W):
        h = G[:, c] * h + X[:, c]; H[:, c] = h
    return {"y": np.stack([H[:, W * r:W * r + W] for r in range(N)]).astype(ml_dtypes.bfloat16)}

@@ -1,0 +1,174 @@
+import comms_topo
+from concourse.bass import DstId, RemoteDMATransfer
+from concourse.mybir import AluOpType, AxisListType, ActivationFunctionType
+
+W = 32
+SLOTS = comms_topo.CORES_PER_CHIP
+PAD = 8
+
+SCRATCH = {
+    "R": ("sbuf", [128, SLOTS, 2 * W], "bfloat16"),
+    "G": ("sbuf", [128, SLOTS * W], "float32"),
+    "X": ("sbuf", [128, SLOTS * W], "bfloat16"),
+    "H": ("sbuf", [128, SLOTS * W], "bfloat16"),
+    "Z": ("sbuf", [128, PAD + W, 2], "float32"),
+    "S": ("sbuf", [128, W + 2], "float32"),
+    "Y": ("sbuf", [128, PAD + W], "bfloat16"),
+    "C": ("sbuf", [128, 8], "bfloat16"),
+}
+SEMAPHORES = ["ld", "raw", "arr", "sent", "sgo", "sg0", "sg1", "cp", "pr", "sc0", "sc1", "fin", "st"]
+
+
+def _bits(mask):
+    return [b for b in range(16) if (mask >> b) & 1]
+
+
+def _count(mask):
+    return len(_bits(mask))
+
+
+def _split(mask, parts):
+    bits = _bits(mask)
+    size = 1
+    while size * 2 * parts <= len(bits):
+        size *= 2
+    return [sum(1 << b for b in bits[i * size:(i + 1) * size]) for i in range(parts)]
+
+
+def _deal(items, hands, topo):
+    out = {h: [] for h in hands}
+    for d in sorted({topo.die(c) for c in items}):
+        hs = [h for h in hands if topo.die(h) == d] or list(hands)
+        for i, c in enumerate([c for c in items if topo.die(c) == d]):
+            out[hs[i % len(hs)]].append(c)
+    return out
+
+
+def _dst(topo, dst, src):
+    rid, pid = topo.addr(dst, src)
+    return DstId(rid=rid, pnc=pid)
+
+
+def rank_program(g, core, T, topo):
+    rank = T.rank_of(core)
+    if rank is None:
+        return
+    sem = T.sem
+    mult, add = AluOpType.mult, AluOpType.add
+    sigmoid = ActivationFunctionType.Sigmoid
+
+    place = lambda c: (topo.host(c), topo.chip(c))
+    up = [c for c in T.cores if place(c) == place(T.cores[0])]
+    down = [c for c in T.cores if place(c) != place(T.cores[0])]
+    porters = [c for c in up if topo.may_write(c, down[0])]
+    far = _deal(down, porters, topo)
+    near = _deal([c for c in up[1:] if c not in porters], porters, topo)
+    mine = up if core in up else down
+    k = mine.index(core)
+    n = len(mine)
+
+    def carry_masks(p):
+        off = topo.mask(p, far[p][0])
+        rest = [topo.mask(p, c) & ~off for c in near[p]]
+        return off, (_split(rest[0], len(rest)) if rest else [])
+
+    g.sync.dma_start(T.R[:, k, 0:W], T.a[:, :]).then_inc(sem.ld, 16)
+    g.scalar.dma_start(T.R[:, k, W:2 * W], T.x[:, :]).then_inc(sem.ld, 16)
+    sent = 0
+
+    if core in up:
+        to = [p for p in porters if p != core]
+        m = topo.mask(core, to[0])
+        g.wait_ge(sem.ld, 32)
+        g.remote_dma_fused([RemoteDMATransfer(dst_ids=[_dst(topo, p, core) for p in to], dma_engine_mask=m,
+                                              remote_sem=sem.raw, srcs=[T.R[:, k, :]], dsts=[T.R[:, k, :] for p in to])],
+                           local_sem=sem.sent)
+        sent += _count(m)
+
+    if core in porters:
+        landed = sum(_count(topo.mask(c, core)) for c in up if c != core)
+        g.scalar.wait_ge(sem.ld, 32)
+        g.scalar.activation(T.G[:, k * W:(k + 1) * W], T.R[:, k, 0:W], sigmoid).then_inc(sem.sgo, 1)
+        g.scalar.wait_ge(sem.raw, landed)
+        half = n // 2
+        parts = [(0, half), (half, n)]
+        calls = []
+        for i, (lo, hi) in enumerate(parts):
+            runs = [(a0, a1) for a0, a1 in ((lo, min(max(k, lo), hi)), (max(min(k + 1, hi), lo), hi)) if a1 > a0]
+            if not lo <= k < hi:
+                runs = [(lo, hi)]
+            for a0, a1 in runs:
+                g.scalar.activation(T.G[:, a0 * W:a1 * W], T.R[:, a0:a1, 0:W], sigmoid).then_inc(sem["sg%d" % i], 1)
+            calls.append(len(runs))
+        g.vector.wait_ge(sem.ld, 32)
+        g.vector.wait_ge(sem.raw, landed)
+        g.vector.tensor_copy(T.X[:, :], T.R[:, :, W:2 * W]).then_inc(sem.cp, 1)
+        g.vector.wait_ge(sem.cp, 1)
+        g.vector.wait_ge(sem.sgo, 1)
+        for i, (lo, hi) in enumerate(parts):
+            g.vector.wait_ge(sem["sg%d" % i], calls[i])
+            if i:
+                g.vector.wait_ge(sem["sc%d" % (i - 1)], 1)
+            cols = slice(lo * W, hi * W)
+            g.vector.tensor_tensor_scan(T.H[:, cols], T.G[:, cols], T.X[:, cols],
+                                        T.H[:, lo * W - 1:lo * W] if i else 0.0, mult, add).then_inc(sem["sc%d" % i], 1)
+        off, rest = carry_masks(core)
+        trs = [RemoteDMATransfer(dst_ids=[_dst(topo, d, core) for d in far[core]], dma_engine_mask=off, remote_sem=sem.arr,
+                                 srcs=[T.H[:, n * W - 1:n * W]], dsts=[T.C[:, 0:1] for d in far[core]])]
+        for c, m in zip(near[core], rest):
+            trs.append(RemoteDMATransfer(dst_ids=[_dst(topo, c, core)], dma_engine_mask=m, remote_sem=sem.arr,
+                                         srcs=[T.H[:, up.index(c) * W - 1:up.index(c) * W]], dsts=[T.C[:, 0:1]]))
+        g.wait_ge(sem.sc0, 1)
+        g.wait_ge(sem.sc1, 1)
+        g.remote_dma_fused(trs, local_sem=sem.sent)
+        sent += _count(off) + sum(_count(m) for m in rest)
+        g.sync.wait_ge(sem["sc%d" % (0 if k < half else 1)], 1)
+        g.sync.dma_start(T.y[:, :], T.H[:, k * W:(k + 1) * W]).then_inc(sem.st, 16)
+        g.sync.wait_ge(sem.st, 16)
+        g.wait_ge(sem.sent, sent)
+        return
+
+    zg, zx = T.Z[:, PAD:PAD + W, 1], T.Z[:, PAD:PAD + W, 0]
+    g.scalar.wait_ge(sem.ld, 32)
+    g.scalar.activation(zg, T.R[:, k, 0:W], sigmoid).then_inc(sem.sgo, 1)
+    g.vector.wait_ge(sem.ld, 32)
+    g.vector.tensor_copy(zx, T.R[:, k, W:2 * W]).then_inc(sem.cp, 1)
+    g.vector.wait_ge(sem.cp, 1)
+    g.vector.wait_ge(sem.sgo, 1)
+
+    before = 0
+    arrive = 0
+    if core in down:
+        before = k
+        arrive += sum(_count(topo.mask(c, core)) for c in down[:k])
+        later = down[k + 1:]
+        if later:
+            g.vector.tensor_tensor_scan(T.S[:, 0:W], zg, zx, 0.0, mult, add).then_inc(sem.pr, 1)
+            g.vector.tensor_reduce(T.S[:, W:W + 1], zg, AxisListType.X, mult).then_inc(sem.pr, 1)
+            m = topo.mask(core, later[0])
+            g.wait_ge(sem.pr, 2)
+            g.remote_dma_fused([RemoteDMATransfer(
+                dst_ids=[_dst(topo, d, core) for d in later], dma_engine_mask=m, remote_sem=sem.arr,
+                srcs=[T.S[:, W - 1:W + 1]],
+                dsts=[T.Z[:, PAD - down.index(d) + k, :] for d in later])], local_sem=sem.sent)
+            sent += _count(m)
+
+    initial = 0.0
+    for p in porters:
+        off, rest = carry_masks(p)
+        if core in far[p]:
+            arrive += _count(off)
+            initial = T.C[:, 0:1]
+        if core in near[p]:
+            arrive += _count(rest[near[p].index(core)])
+            initial = T.C[:, 0:1]
+    if arrive:
+        g.vector.wait_ge(sem.arr, arrive)
+    lo = PAD - before
+    g.vector.tensor_tensor_scan(T.Y[:, lo:PAD + W], T.Z[:, lo:PAD + W, 1], T.Z[:, lo:PAD + W, 0], initial, mult, add
+                                ).then_inc(sem.fin, 1)
+    g.sync.wait_ge(sem.fin, 1)
+    g.sync.dma_start(T.y[:, :], T.Y[:, PAD:PAD + W]).then_inc(sem.st, 16)
+    g.sync.wait_ge(sem.st, 16)
+    if sent:
+        g.wait_ge(sem.sent, sent)

@@ -7,16 +7,18 @@ SLOTS = comms_topo.CORES_PER_CHIP
 PAD = 8
 
 SCRATCH = {
-    "R": ("sbuf", [128, SLOTS, 2 * W], "bfloat16"),
+    "DA": ("dram", [128, W], "bfloat16"),
+    "DX": ("dram", [128, W], "bfloat16"),
+    "RA": ("sbuf", [128, SLOTS * W], "bfloat16"),
+    "RX": ("sbuf", [128, SLOTS * W], "bfloat16"),
     "G": ("sbuf", [128, SLOTS * W], "float32"),
-    "X": ("sbuf", [128, SLOTS * W], "bfloat16"),
     "H": ("sbuf", [128, SLOTS * W], "bfloat16"),
     "Z": ("sbuf", [128, PAD + W, 2], "float32"),
     "S": ("sbuf", [128, W + 2], "float32"),
     "Y": ("sbuf", [128, PAD + W], "bfloat16"),
     "C": ("sbuf", [128, 8], "bfloat16"),
 }
-SEMAPHORES = ["ld", "raw", "arr", "sent", "sgo", "sg0", "sg1", "cp", "pr", "sc0", "sc1", "fin", "st"]
+SEMAPHORES = ["sa", "sx", "la", "lx", "rawa", "rawx", "arr", "sent", "sgo", "sg", "cp", "pr", "sc", "fin", "st"]
 
 
 def _bits(mask):
@@ -66,73 +68,63 @@ def rank_program(g, core, T, topo):
     mine = up if core in up else down
     k = mine.index(core)
     n = len(mine)
+    own = slice(k * W, (k + 1) * W)
 
     def carry_masks(p):
         off = topo.mask(p, far[p][0])
         rest = [topo.mask(p, c) & ~off for c in near[p]]
         return off, (_split(rest[0], len(rest)) if rest else [])
 
-    g.sync.dma_start(T.R[:, k, 0:W], T.a[:, :]).then_inc(sem.ld, 16)
-    g.scalar.dma_start(T.R[:, k, W:2 * W], T.x[:, :]).then_inc(sem.ld, 16)
+    if core in up:
+        g.sync.dma_start(T.DA[:, :], T.a[:, :]).then_inc(sem.sa, 16)
+        g.scalar.dma_start(T.DX[:, :], T.x[:, :]).then_inc(sem.sx, 16)
+    g.sync.dma_start(T.RA[:, own], T.a[:, :]).then_inc(sem.la, 16)
+    g.scalar.dma_start(T.RX[:, own], T.x[:, :]).then_inc(sem.lx, 16)
     sent = 0
 
     if core in up:
         to = [p for p in porters if p != core]
         m = topo.mask(core, to[0])
-        g.wait_ge(sem.ld, 32)
-        g.remote_dma_fused([RemoteDMATransfer(dst_ids=[_dst(topo, p, core) for p in to], dma_engine_mask=m,
-                                              remote_sem=sem.raw, srcs=[T.R[:, k, :]], dsts=[T.R[:, k, :] for p in to])],
-                           local_sem=sem.sent)
-        sent += _count(m)
+        for ready, src, buf, land in ((sem.sa, T.DA, T.RA, sem.rawa), (sem.sx, T.DX, T.RX, sem.rawx)):
+            g.wait_ge(ready, 16)
+            g.remote_dma_fused([RemoteDMATransfer(dst_ids=[_dst(topo, p, core) for p in to], dma_engine_mask=m,
+                                                  remote_sem=land, srcs=[src[:, :]], dsts=[buf[:, own] for p in to])],
+                               local_sem=sem.sent)
+            sent += _count(m)
 
     if core in porters:
         landed = sum(_count(topo.mask(c, core)) for c in up if c != core)
-        g.scalar.wait_ge(sem.ld, 32)
-        g.scalar.activation(T.G[:, k * W:(k + 1) * W], T.R[:, k, 0:W], sigmoid).then_inc(sem.sgo, 1)
-        g.scalar.wait_ge(sem.raw, landed)
-        half = n // 2
-        parts = [(0, half), (half, n)]
-        calls = []
-        for i, (lo, hi) in enumerate(parts):
-            runs = [(a0, a1) for a0, a1 in ((lo, min(max(k, lo), hi)), (max(min(k + 1, hi), lo), hi)) if a1 > a0]
-            if not lo <= k < hi:
-                runs = [(lo, hi)]
-            for a0, a1 in runs:
-                g.scalar.activation(T.G[:, a0 * W:a1 * W], T.R[:, a0:a1, 0:W], sigmoid).then_inc(sem["sg%d" % i], 1)
-            calls.append(len(runs))
-        g.vector.wait_ge(sem.ld, 32)
-        g.vector.wait_ge(sem.raw, landed)
-        g.vector.tensor_copy(T.X[:, :], T.R[:, :, W:2 * W]).then_inc(sem.cp, 1)
-        g.vector.wait_ge(sem.cp, 1)
+        g.scalar.wait_ge(sem.la, 16)
+        g.scalar.activation(T.G[:, own], T.RA[:, own], sigmoid).then_inc(sem.sgo, 1)
+        g.scalar.wait_ge(sem.rawa, landed)
+        runs = [(a0, a1) for a0, a1 in ((0, k), (k + 1, n)) if a1 > a0]
+        for a0, a1 in runs:
+            g.scalar.activation(T.G[:, a0 * W:a1 * W], T.RA[:, a0 * W:a1 * W], sigmoid).then_inc(sem.sg, 1)
+        g.vector.wait_ge(sem.lx, 16)
         g.vector.wait_ge(sem.sgo, 1)
-        for i, (lo, hi) in enumerate(parts):
-            g.vector.wait_ge(sem["sg%d" % i], calls[i])
-            if i:
-                g.vector.wait_ge(sem["sc%d" % (i - 1)], 1)
-            cols = slice(lo * W, hi * W)
-            g.vector.tensor_tensor_scan(T.H[:, cols], T.G[:, cols], T.X[:, cols],
-                                        T.H[:, lo * W - 1:lo * W] if i else 0.0, mult, add).then_inc(sem["sc%d" % i], 1)
+        g.vector.wait_ge(sem.sg, len(runs))
+        g.vector.wait_ge(sem.rawx, landed)
+        g.vector.tensor_tensor_scan(T.H[:, :], T.G[:, :], T.RX[:, :], 0.0, mult, add).then_inc(sem.sc, 2)
         off, rest = carry_masks(core)
         trs = [RemoteDMATransfer(dst_ids=[_dst(topo, d, core) for d in far[core]], dma_engine_mask=off, remote_sem=sem.arr,
                                  srcs=[T.H[:, n * W - 1:n * W]], dsts=[T.C[:, 0:1] for d in far[core]])]
         for c, m in zip(near[core], rest):
             trs.append(RemoteDMATransfer(dst_ids=[_dst(topo, c, core)], dma_engine_mask=m, remote_sem=sem.arr,
                                          srcs=[T.H[:, up.index(c) * W - 1:up.index(c) * W]], dsts=[T.C[:, 0:1]]))
-        g.wait_ge(sem.sc0, 1)
-        g.wait_ge(sem.sc1, 1)
+        g.wait_ge(sem.sc, 2)
         g.remote_dma_fused(trs, local_sem=sem.sent)
         sent += _count(off) + sum(_count(m) for m in rest)
-        g.sync.wait_ge(sem["sc%d" % (0 if k < half else 1)], 1)
-        g.sync.dma_start(T.y[:, :], T.H[:, k * W:(k + 1) * W]).then_inc(sem.st, 16)
+        g.sync.wait_ge(sem.sc, 2)
+        g.sync.dma_start(T.y[:, :], T.H[:, own]).then_inc(sem.st, 16)
         g.sync.wait_ge(sem.st, 16)
         g.wait_ge(sem.sent, sent)
         return
 
     zg, zx = T.Z[:, PAD:PAD + W, 1], T.Z[:, PAD:PAD + W, 0]
-    g.scalar.wait_ge(sem.ld, 32)
-    g.scalar.activation(zg, T.R[:, k, 0:W], sigmoid).then_inc(sem.sgo, 1)
-    g.vector.wait_ge(sem.ld, 32)
-    g.vector.tensor_copy(zx, T.R[:, k, W:2 * W]).then_inc(sem.cp, 1)
+    g.scalar.wait_ge(sem.la, 16)
+    g.scalar.activation(zg, T.RA[:, own], sigmoid).then_inc(sem.sgo, 1)
+    g.vector.wait_ge(sem.lx, 16)
+    g.vector.tensor_copy(zx, T.RX[:, own]).then_inc(sem.cp, 1)
     g.vector.wait_ge(sem.cp, 1)
     g.vector.wait_ge(sem.sgo, 1)
 

import comms_topo
from concourse.bass import DstId, RemoteDMATransfer
from concourse.mybir import AluOpType, AxisListType, ActivationFunctionType

W = 32
SLOTS = comms_topo.CORES_PER_CHIP
PAD = 8

SCRATCH = {
    "DA": ("dram", [128, W], "bfloat16"),
    "DX": ("dram", [128, W], "bfloat16"),
    "RA": ("sbuf", [128, SLOTS * W], "bfloat16"),
    "RX": ("sbuf", [128, SLOTS * W], "bfloat16"),
    "G": ("sbuf", [128, SLOTS * W], "float32"),
    "H": ("sbuf", [128, SLOTS * W], "bfloat16"),
    "Z": ("sbuf", [128, PAD + W, 2], "float32"),
    "S": ("sbuf", [128, W + 2], "float32"),
    "Y": ("sbuf", [128, PAD + W], "bfloat16"),
    "C": ("sbuf", [128, 8], "bfloat16"),
}
SEMAPHORES = ["sa", "sx", "la", "lx", "rawa", "rawx", "arr", "sent", "sgo", "sg", "cp", "pr", "sc", "fin", "st"]


def _bits(mask):
    return [b for b in range(16) if (mask >> b) & 1]


def _count(mask):
    return len(_bits(mask))


def _split(mask, parts):
    bits = _bits(mask)
    size = 1
    while size * 2 * parts <= len(bits):
        size *= 2
    return [sum(1 << b for b in bits[i * size:(i + 1) * size]) for i in range(parts)]


def _deal(items, hands, topo):
    out = {h: [] for h in hands}
    for d in sorted({topo.die(c) for c in items}):
        hs = [h for h in hands if topo.die(h) == d] or list(hands)
        for i, c in enumerate([c for c in items if topo.die(c) == d]):
            out[hs[i % len(hs)]].append(c)
    return out


def _dst(topo, dst, src):
    rid, pid = topo.addr(dst, src)
    return DstId(rid=rid, pnc=pid)


def rank_program(g, core, T, topo):
    rank = T.rank_of(core)
    if rank is None:
        return
    sem = T.sem
    mult, add = AluOpType.mult, AluOpType.add
    sigmoid = ActivationFunctionType.Sigmoid

    place = lambda c: (topo.host(c), topo.chip(c))
    up = [c for c in T.cores if place(c) == place(T.cores[0])]
    down = [c for c in T.cores if place(c) != place(T.cores[0])]
    porters = [c for c in up if topo.may_write(c, down[0])]
    far = _deal(down, porters, topo)
    near = _deal([c for c in up[1:] if c not in porters], porters, topo)
    mine = up if core in up else down
    k = mine.index(core)
    n = len(mine)
    own = slice(k * W, (k + 1) * W)

    def carry_masks(p):
        off = topo.mask(p, far[p][0])
        rest = [topo.mask(p, c) & ~off for c in near[p]]
        return off, (_split(rest[0], len(rest)) if rest else [])

    if core in up:
        g.sync.dma_start(T.DA[:, :], T.a[:, :]).then_inc(sem.sa, 16)
        g.scalar.dma_start(T.DX[:, :], T.x[:, :]).then_inc(sem.sx, 16)
    g.sync.dma_start(T.RA[:, own], T.a[:, :]).then_inc(sem.la, 16)
    g.scalar.dma_start(T.RX[:, own], T.x[:, :]).then_inc(sem.lx, 16)
    sent = 0

    if core in up:
        to = [p for p in porters if p != core]
        m = topo.mask(core, to[0])
        for ready, src, buf, land in ((sem.sa, T.DA, T.RA, sem.rawa), (sem.sx, T.DX, T.RX, sem.rawx)):
            g.wait_ge(ready, 16)
            g.remote_dma_fused([RemoteDMATransfer(dst_ids=[_dst(topo, p, core) for p in to], dma_engine_mask=m,
                                                  remote_sem=land, srcs=[src[:, :]], dsts=[buf[:, own] for p in to])],
                               local_sem=sem.sent)
            sent += _count(m)

    if core in porters:
        landed = sum(_count(topo.mask(c, core)) for c in up if c != core)
        g.scalar.wait_ge(sem.la, 16)
        g.scalar.activation(T.G[:, own], T.RA[:, own], sigmoid).then_inc(sem.sgo, 1)
        g.scalar.wait_ge(sem.rawa, landed)
        runs = [(a0, a1) for a0, a1 in ((0, k), (k + 1, n)) if a1 > a0]
        for a0, a1 in runs:
            g.scalar.activation(T.G[:, a0 * W:a1 * W], T.RA[:, a0 * W:a1 * W], sigmoid).then_inc(sem.sg, 1)
        g.vector.wait_ge(sem.lx, 16)
        g.vector.wait_ge(sem.sgo, 1)
        g.vector.wait_ge(sem.sg, len(runs))
        g.vector.wait_ge(sem.rawx, landed)
        g.vector.tensor_tensor_scan(T.H[:, :], T.G[:, :], T.RX[:, :], 0.0, mult, add).then_inc(sem.sc, 2)
        off, rest = carry_masks(core)
        trs = [RemoteDMATransfer(dst_ids=[_dst(topo, d, core) for d in far[core]], dma_engine_mask=off, remote_sem=sem.arr,
                                 srcs=[T.H[:, n * W - 1:n * W]], dsts=[T.C[:, 0:1] for d in far[core]])]
        for c, m in zip(near[core], rest):
            trs.append(RemoteDMATransfer(dst_ids=[_dst(topo, c, core)], dma_engine_mask=m, remote_sem=sem.arr,
                                         srcs=[T.H[:, up.index(c) * W - 1:up.index(c) * W]], dsts=[T.C[:, 0:1]]))
        g.wait_ge(sem.sc, 2)
        g.remote_dma_fused(trs, local_sem=sem.sent)
        sent += _count(off) + sum(_count(m) for m in rest)
        g.sync.wait_ge(sem.sc, 2)
        g.sync.dma_start(T.y[:, :], T.H[:, own]).then_inc(sem.st, 16)
        g.sync.wait_ge(sem.st, 16)
        g.wait_ge(sem.sent, sent)
        return

    zg, zx = T.Z[:, PAD:PAD + W, 1], T.Z[:, PAD:PAD + W, 0]
    g.scalar.wait_ge(sem.la, 16)
    g.scalar.activation(zg, T.RA[:, own], sigmoid).then_inc(sem.sgo, 1)
    g.vector.wait_ge(sem.lx, 16)
    g.vector.tensor_copy(zx, T.RX[:, own]).then_inc(sem.cp, 1)
    g.vector.wait_ge(sem.cp, 1)
    g.vector.wait_ge(sem.sgo, 1)

    before = 0
    arrive = 0
    if core in down:
        before = k
        arrive += sum(_count(topo.mask(c, core)) for c in down[:k])
        later = down[k + 1:]
        if later:
            g.vector.tensor_tensor_scan(T.S[:, 0:W], zg, zx, 0.0, mult, add).then_inc(sem.pr, 1)
            g.vector.tensor_reduce(T.S[:, W:W + 1], zg, AxisListType.X, mult).then_inc(sem.pr, 1)
            m = topo.mask(core, later[0])
            g.wait_ge(sem.pr, 2)
            g.remote_dma_fused([RemoteDMATransfer(
                dst_ids=[_dst(topo, d, core) for d in later], dma_engine_mask=m, remote_sem=sem.arr,
                srcs=[T.S[:, W - 1:W + 1]],
                dsts=[T.Z[:, PAD - down.index(d) + k, :] for d in later])], local_sem=sem.sent)
            sent += _count(m)

    initial = 0.0
    for p in porters:
        off, rest = carry_masks(p)
        if core in far[p]:
            arrive += _count(off)
            initial = T.C[:, 0:1]
        if core in near[p]:
            arrive += _count(rest[near[p].index(core)])
            initial = T.C[:, 0:1]
    if arrive:
        g.vector.wait_ge(sem.arr, arrive)
    lo = PAD - before
    g.vector.tensor_tensor_scan(T.Y[:, lo:PAD + W], T.Z[:, lo:PAD + W, 1], T.Z[:, lo:PAD + W, 0], initial, mult, add
                                ).then_inc(sem.fin, 1)
    g.sync.wait_ge(sem.fin, 1)
    g.sync.dma_start(T.y[:, :], T.Y[:, PAD:PAD + W]).then_inc(sem.st, 16)
    g.sync.wait_ge(sem.st, 16)
    if sent:
        g.wait_ge(sem.sent, sent)
